import numpy as np
import ml_dtypes


def mxq(x, axis, fmt="e4m3"):
    dtype, down = {"e4m3": (ml_dtypes.float8_e4m3fn, 7), "e5m2": (ml_dtypes.float8_e5m2, 14)}[fmt]
    v = np.moveaxis(np.asarray(x, np.float32).astype(ml_dtypes.bfloat16).astype(np.float64), axis, -1)
    blocks = v.reshape(v.shape[:-1] + (-1, 32))
    amax = np.abs(blocks).max(-1, keepdims=True)
    byte = np.maximum(np.where(amax > 0, np.frexp(amax)[1] - 1 + 127, 0) - down, 1)
    scale = np.exp2(byte - 127.0)
    codes = (blocks / scale).astype(np.float32).astype(dtype).astype(np.float64)
    return np.moveaxis((codes * scale).reshape(v.shape), -1, axis)


WIDE = False


def mx_kscale(k):
    if not WIDE:
        return np.ones(k)
    levels = np.array([10, -10, 5, -5, 0])
    if k % 512:
        return np.exp2(np.random.permutation(np.resize(levels, k // 32))).repeat(32)
    a = np.empty((k // 512, 16))
    for p in range(k // 512):
        a[p, :8] = np.random.permutation(np.resize(levels, 8))
        for g in range(8):
            far = levels[np.abs(levels - a[p, g]) >= 10]
            a[p, g + 8] = far[np.random.randint(len(far))]
    return np.exp2(a.ravel()).repeat(32)


BF16 = ml_dtypes.bfloat16


def bf(x):
    return np.asarray(x, np.float32).astype(BF16)


def f64(x):
    return np.asarray(x).astype(np.float64)


E2M1 = np.array([0.0, 0.5, 1.0, 1.5, 2.0, 3.0, 4.0, 6.0, -0.0, -0.5, -1.0, -1.5, -2.0, -3.0, -4.0, -6.0])


def pack_weight(w, fmt):
    k, n = w.shape
    w = f64(bf(w)).reshape(k // 32, 32, n)
    amax = np.abs(w).max(1)
    if fmt == "e4m3":
        byte = np.frexp(amax)[1] - 1 + 127 - 7
    else:
        mant, ex = np.frexp(amax / 6.0)
        byte = np.where(mant > 0.5, ex, ex - 1) + 127
    byte = np.clip(np.where(amax > 0, byte, 1), 1, 254)
    scaled = (w * np.exp2(127.0 - byte)[:, None, :]).reshape(k, n).astype(np.float32)
    by_word = np.ascontiguousarray(scaled.reshape(k // 512, 128, 4, n).transpose(0, 1, 3, 2))
    if fmt == "e4m3":
        words = by_word.astype(ml_dtypes.float8_e4m3fn).view(np.uint8)
    else:
        c = by_word.astype(ml_dtypes.float4_e2m1fn).view(np.uint8) & 0xF
        words = c[..., 0::2] | (c[..., 1::2] << 4)
    return np.ascontiguousarray(words), np.ascontiguousarray(byte.astype(np.uint8).reshape(k // 512, 16, n))


def unpack_weight(words, scales, fmt):
    g, p, n, _ = words.shape
    if fmt == "e4m3":
        vals = np.ascontiguousarray(words).view(ml_dtypes.float8_e4m3fn).astype(np.float64)
    else:
        nib = np.empty((g, p, n, 4), np.uint8)
        nib[..., 0::2] = words & 0xF
        nib[..., 1::2] = words >> 4
        vals = E2M1[nib]
    vals = vals * np.repeat(np.exp2(scales.astype(np.float64) - 127.0), 8, axis=1)[..., None]
    return vals.transpose(0, 1, 3, 2).reshape(g * 512, n)
def pack4(w):
    words, scales = pack_weight(w, "e2m1")
    return words.reshape(words.shape[0], 128, -1), scales


def unpack4(words, scales):
    return unpack_weight(words.reshape(words.shape[0], 128, -1, 2), scales, "e2m1")


def planes(Y):
    n, m = Y.shape
    b = f64(bf(Y)).reshape(n // 32, 32, m)
    amax = np.abs(b).max(1)
    byte = np.clip(np.where(amax > 0, np.frexp(amax)[1] - 1 + 127 - 7, 1), 1, 254)
    codes = (b * np.exp2(127.0 - byte)[:, None, :]).reshape(n, m).astype(np.float32).astype(ml_dtypes.float8_e4m3fn).view(np.uint8)
    words = codes.reshape(n // 512, 128, 4, m).transpose(0, 1, 3, 2)
    return np.ascontiguousarray(words), np.ascontiguousarray(byte.astype(np.uint8).reshape(n // 512, 16, m))


G, P, T, D, N = 4, 1024, 1024, 512, 512

RS = 1.0 / np.sqrt(D)


def setup_inputs():
    s = mx_kscale(G * D).reshape(G, 1, D)
    t = mx_kscale(G * T).reshape(G, T)
    src_feat = np.random.randn(G, P, D) * s
    tgt_feat = np.random.randn(G, T, D) / s
    tgt_gain = (1.0 + 0.2 * np.random.randn(G, T)) * t
    pool = np.random.randn(G * T, N) / np.sqrt(T) / t.reshape(G * T, 1)
    pool_words, pool_scales = pack4(pool)
    return {
        "src_feat": bf(src_feat),
        "tgt_feat": bf(tgt_feat),
        "tgt_gain": bf(tgt_gain),
        "pool_words": pool_words,
        "pool_scales": pool_scales,
        "cell_bias": bf(0.3 * np.random.randn(G, N)),
        "cell_gain": bf(np.exp(0.8 * np.random.randn(G, N))),
        "src_gain": bf(1.0 + 0.2 * np.random.randn(G, P)),
    }


def reference(src_feat, tgt_feat, tgt_gain, pool_words, pool_scales, cell_bias, cell_gain, src_gain):
    a = mxq(f64(src_feat), 2, "e4m3")
    b = mxq(f64(tgt_feat), 2, "e4m3")
    corr = a @ b.swapaxes(1, 2)
    corr = corr * RS * f64(tgt_gain)[:, None, :]
    pool = unpack4(pool_words, pool_scales).reshape(G, T, N)
    pooled = mxq(corr, 2, "e4m3") @ pool
    y = (pooled + f64(cell_bias)[:, None, :]) * f64(cell_gain)[:, None, :] * f64(src_gain)[:, :, None]
    Y = y.reshape(G * P, N).T
    words, scales = planes(Y)
    return y, words, scales

@@ -1,0 +1,353 @@
+import math
+from contextlib import ExitStack
+
+import concourse.mybir as mybir
+from concourse.masks import make_identity
+
+G, SRC, TGT, D, CELLS = 4, 1024, 1024, 512, 512
+FLOPS = 2 * G * SRC * TGT * D + 2 * G * SRC * TGT * CELLS
+
+F32 = mybir.dt.float32
+BF16 = mybir.dt.bfloat16
+I32 = mybir.dt.int32
+U32 = mybir.dt.uint32
+U8 = mybir.dt.uint8
+FP8X4 = mybir.dt.float8_e4m3fn_x4
+FP4X4 = mybir.dt.float4_e2m1fn_x4
+ACT = mybir.ActivationFunctionType
+ALU = mybir.AluOpType
+
+P = 128
+PACK = 4
+SPAN = P * PACK
+HALVES = 2 * G
+STEPS = 2 * HALVES
+GROUPED_BUFS = 7
+TURN = (4, 4, 3, 3, 2, 1, 2, 1, 2, 1, 2, 1, 1, 1, 0, 0)
+GCOLS = 192
+EARLY = 3
+PERM = {0: (2, 3, 8), 1: (9, 10, 11), 2: (4, 5), 3: (6, 7)}
+RS = 1.0 / math.sqrt(D)
+
+
+def tile_grouped_correlation_dense_pooling_k7_kernel(
+    tc, src_feat, tgt_feat, tgt_gain, pool_words, pool_scales, cell_bias, cell_gain, src_gain, out_0, out_1, out_2
+):
+    nc = tc.nc
+    with ExitStack() as ctx:
+        keep = ctx.enter_context(tc.tile_pool(name="keep", bufs=1))
+        work = ctx.enter_context(tc.tile_pool(name="work", bufs=2))
+        psum = ctx.enter_context(tc.psum_pool(name="psum", bufs=4))
+        ctx.enter_context(tc.manual_schedule())
+
+        ident = keep.tile([P, P], F32, name="ident")
+        make_identity(nc, ident[:])
+        pool_scale_raw = keep.tile([P, HALVES, CELLS], U8, name="pool_scale_raw", align_bytes=64)
+        nc.gpsimd.memset(pool_scale_raw[:].rearrange("p g n -> p (g n)").bitcast(I32), 0)
+        gain_rows = keep.tile([P, P], BF16, name="gain_rows")
+        nc.gpsimd.memset(gain_rows[:], 0.0)
+
+        raw = {}
+
+        def load_unit(u, parts=1):
+            h, kind = divmod(u, 4)
+            rows = slice(SPAN * (kind // 2), SPAN * (kind // 2 + 1))
+            raw[u] = work.tile([P, PACK, D], BF16, name="raw", bufs=12)
+            if kind % 2 == 0:
+                view = tgt_feat[h, rows, :].rearrange("(m s) k -> m s k", s=PACK)
+            else:
+                view = src_feat[h, rows, :].rearrange("(s m) k -> m s k", s=PACK)
+            step = PACK // parts
+            for s in range(0, PACK, step):
+                nc.sync.dma_start(out=raw[u][:, s : s + step, :], in_=view[:, s : s + step, :])
+
+        pool_raw = keep.tile([P, HALVES, 2 * CELLS], U8, name="pool_raw", align_bytes=64)
+        tgain = keep.tile([P, HALVES, PACK], BF16, name="tgain")
+        cbias = keep.tile([P, G, PACK], BF16, name="cbias")
+        cgain = keep.tile([P, G, PACK], BF16, name="cgain")
+        sgain_all = keep.tile([P, G * SRC], BF16, name="sgain_all")
+
+        def load_pool_words(g0, g1):
+            nc.sync.dma_start(
+                out=pool_raw[:, g0:g1, :].bitcast(I32),
+                in_=pool_words[g0:g1].rearrange("g p n -> p g n").bitcast(I32),
+            )
+
+        load_unit(0, 2)
+        load_pool_words(0, 2)
+        load_unit(1, 2)
+        nc.sync.dma_start(out=tgain[:], in_=tgt_gain.rearrange("h (g p t) -> p (h g) t", p=P, t=PACK))
+        load_unit(2)
+        load_pool_words(2, 4)
+        for q in range(4):
+            nc.sync.dma_start(
+                out=pool_scale_raw[32 * q : 32 * q + 4, :, :].bitcast(I32),
+                in_=pool_scales[:, 4 * q : 4 * q + 4, :].rearrange("g r n -> r g n").bitcast(I32),
+            )
+        nc.sync.dma_start(out=cbias[:], in_=cell_bias.rearrange("h (p t) -> p h t", t=PACK))
+        nc.sync.dma_start(out=cgain[:], in_=cell_gain.rearrange("h (p t) -> p h t", t=PACK))
+        nc.sync.dma_start(out=gain_rows[0:32, :], in_=src_gain.rearrange("h (b m) -> (h b) m", m=P))
+        load_unit(3)
+        load_unit(4)
+        load_pool_words(4, 8)
+        load_unit(5)
+        for h in range(G):
+            nc.sync.dma_start(out=sgain_all[:, SRC * h : SRC * (h + 1)], in_=src_gain[h].partition_broadcast(P))
+            for u in range(6 + 3 * h, min(9 + 3 * h, 4 * G)):
+                load_unit(u)
+
+        pool_codes = keep.tile([P, HALVES, 2 * CELLS], U8, name="pool_codes", align_bytes=64)
+        pool_scale = keep.tile([P, HALVES, CELLS], U8, name="pool_scale", align_bytes=64)
+        out_codes = keep.tile([P, G * SRC], U32, name="out_codes", align_bytes=64)
+        out_scale = keep.tile([P, G * SRC], U8, name="out_scale", align_bytes=64)
+        tgain32 = keep.tile([P, HALVES, PACK], F32, name="tgain32")
+        cgain32 = keep.tile([P, G, PACK], F32, name="cgain32")
+        cshift32 = keep.tile([P, G, PACK], F32, name="cshift32")
+        gain_rows32 = keep.tile([P, P], F32, name="gain_rows32")
+        sgain_col = keep.tile([P, 32], F32, name="sgain_col")
+
+        def permute_pool(j):
+            if j < HALVES:
+                g = j
+                nc.vector.tensor_copy(
+                    out=pool_codes[:, g, :].rearrange("p (t m b) -> p t m b", t=PACK, b=2),
+                    in_=pool_raw[:, g, :].rearrange("p (m t b) -> p t m b", t=PACK, b=2),
+                )
+            else:
+                h = j - HALVES
+                nc.vector.tensor_copy(
+                    out=pool_scale[:, 2 * h : 2 * h + 2, :].rearrange("p g (t m) -> p g t m", t=PACK),
+                    in_=pool_scale_raw[:, 2 * h : 2 * h + 2, :].rearrange("p g (m t) -> p g t m", t=PACK),
+                )
+
+        grouped, feat_codes, feat_scale = {}, {}, {}
+
+        def turn_banks(first_bank, last_bank):
+            for j in range(first_bank, last_bank):
+                u, b = divmod(j, 2)
+                words = raw[u][:].rearrange("p s k -> p (s k)").bitcast(F32)
+                if b == 0:
+                    grouped[u] = work.tile([P, SPAN * PACK], BF16, name="grouped", bufs=GROUPED_BUFS, align_bytes=64)
+                pairs = grouped[u][:].bitcast(F32).rearrange("p (c e) -> p c e", e=2)
+                bank = psum.tile([P, 2, 2 * P], F32, name="sbank")
+                for s in range(2):
+                    for e in range(2):
+                        first = (2 * b + s) * (D // 2) + e
+                        nc.tensor.transpose(
+                            bank[:, e, s * P : (s + 1) * P], words[:, first : first + D // 2 - e : 2], ident[:]
+                        )
+                nc.scalar.copy(out=pairs[:, 2 * P * b : 2 * P * (b + 1), :], in_=bank[:].rearrange("p e c -> p c e"))
+
+        def quantize_unit(u, parts=1):
+            feat_codes[u] = work.tile([P, SPAN], U32, name="feat_codes", bufs=6, align_bytes=64)
+            feat_scale[u] = work.tile([P, SPAN], U8, name="feat_scale", bufs=6, align_bytes=64)
+            step = SPAN // parts
+            for c in range(0, SPAN, step):
+                nc.vector.quantize_mx(
+                    out=feat_codes[u][:, c : c + step].bitcast(FP8X4),
+                    scales=feat_scale[u][:, c : c + step],
+                    in_=grouped[u][:, PACK * c : PACK * (c + step)],
+                )
+
+        corr, corr_codes, corr_scale = {}, {}, {}
+
+        def correlate(k, by_scalar):
+            n, g = divmod(k, 2)
+            h, half = divmod(n, 2)
+            ut, us = 4 * h + 2 * g, 4 * h + 2 * half + 1
+            corr[k] = work.tile([P, SPAN, PACK], BF16, name="corr", bufs=2, align_bytes=64)
+            for b in range(4):
+                cols = slice(P * b, P * (b + 1))
+                bank = psum.tile([P, PACK, P], F32, name="vbank")
+                for t in range(PACK):
+                    tcols = slice(P * t, P * (t + 1))
+                    nc.tensor.matmul_mx(
+                        out=bank[:, t, :],
+                        lhsT=feat_codes[ut][:, tcols].bitcast(FP8X4),
+                        lhsT_scale=feat_scale[ut][:, tcols],
+                        rhs=feat_codes[us][:, cols].bitcast(FP8X4),
+                        rhs_scale=feat_scale[us][:, cols],
+                        start=True,
+                        stop=True,
+                    )
+                if b in by_scalar:
+                    for t in range(PACK):
+                        nc.scalar.activation(
+                            out=corr[k][:, cols, t],
+                            in_=bank[:, t, :],
+                            func=ACT.Copy,
+                            scale=tgain32[:, 2 * h + g, t : t + 1],
+                        )
+                    continue
+                nc.vector.scalar_tensor_tensor(
+                    out=corr[k][:, cols, :],
+                    in0=bank[:].rearrange("p t i -> p i t"),
+                    scalar=RS,
+                    in1=tgain[:, 2 * h + g, :].unsqueeze(1).to_broadcast([P, P, PACK]),
+                    op0=ALU.mult,
+                    op1=ALU.mult,
+                )
+
+        def quantize_corr(k):
+            corr_codes[k] = work.tile([P, SPAN], U32, name="corr_codes", bufs=4, align_bytes=64)
+            corr_scale[k] = work.tile([P, SPAN], U8, name="corr_scale", bufs=4, align_bytes=64)
+            nc.vector.quantize_mx(
+                out=corr_codes[k][:].bitcast(FP8X4),
+                scales=corr_scale[k][:],
+                in_=corr[k][:].rearrange("p i t -> p (i t)"),
+            )
+
+        pooled = {}
+
+        def pool_cells(n, t):
+            h = n // 2
+            if t == 0:
+                pooled[n] = work.tile([P, PACK, SPAN], F32, name="pooled", bufs=3)
+            bank = psum.tile([P, SPAN], F32, name="sbank")
+            for g in range(2):
+                nc.tensor.matmul_mx(
+                    out=bank[:],
+                    lhsT=pool_codes[:, 2 * h + g, 2 * P * t : 2 * P * (t + 1)].bitcast(FP4X4),
+                    lhsT_scale=pool_scale[:, 2 * h + g, P * t : P * (t + 1)],
+                    rhs=corr_codes[2 * n + g][:].bitcast(FP8X4),
+                    rhs_scale=corr_scale[2 * n + g][:],
+                    start=(g == 0),
+                    stop=(g == 1),
+                )
+            nc.scalar.activation(
+                out=pooled[n][:, t, :],
+                in_=bank[:],
+                func=ACT.Identity,
+                bias=cshift32[:, h, t : t + 1],
+                scale=cgain32[:, h, t : t + 1],
+            )
+
+        def store_rows(c, whole=True):
+            n, part = divmod(c, 2)
+            y = work.tile([P, 2, CELLS], F32, name="y", bufs=5)
+            for s in range(2):
+                b = 2 * part + s
+                bank = psum.tile([P, PACK, P], F32, name="sbank")
+                for t in range(PACK):
+                    nc.tensor.transpose(bank[:, t, :], pooled[n][:, t, P * b : P * (b + 1)], ident[:])
+                nc.scalar.activation(
+                    out=y[:, s, :].rearrange("i (p t) -> i p t", t=PACK),
+                    in_=bank[:].rearrange("i t p -> i p t"),
+                    func=ACT.Copy,
+                    scale=sgain_col[:, 4 * n + b : 4 * n + b + 1],
+                )
+                h, first = divmod(2 * P * c, SRC)
+                if not whole:
+                    nc.sync.dma_start(out=out_0[h, first + P * s : first + P * (s + 1), :], in_=y[:, s, :])
+            if whole:
+                nc.sync.dma_start(
+                    out=out_0[h, first : first + 2 * P, :].rearrange("(s m) c -> m s c", s=2), in_=y[:]
+                )
+
+        rounded = {}
+
+        def round_chunk(c, engine, name, bufs, first=0, last=2 * P):
+            n, part = divmod(c, 2)
+            if first == 0:
+                rounded[c] = work.tile([P, 2 * P, PACK], BF16, name=name, bufs=bufs, align_bytes=64)
+            engine.tensor_tensor(
+                out=rounded[c][:, first:last, :],
+                in0=pooled[n][:, :, 2 * P * part + first : 2 * P * part + last].rearrange("p t i -> p i t"),
+                in1=sgain_all[:, 2 * P * c + first : 2 * P * c + last].unsqueeze(2).to_broadcast([P, last - first, PACK]),
+                op=ALU.mult,
+            )
+
+        words_out = out_1[0].rearrange("p m t -> p (m t)").bitcast(I32)
+
+        def quantize_chunk(c):
+            cols = slice(2 * P * c, 2 * P * (c + 1))
+            nc.vector.quantize_mx(
+                out=out_codes[:, cols].bitcast(FP8X4),
+                scales=out_scale[:, cols],
+                in_=rounded[c][:].rearrange("p i t -> p (i t)"),
+            )
+
+        def store_words(first, last):
+            cols = slice(2 * P * first, 2 * P * last)
+            nc.sync.dma_start(out=words_out[:, cols], in_=out_codes[:, cols].bitcast(I32))
+
+        def store_scales(first, last, engines):
+            for q in range(4):
+                engines[q].dma_start(
+                    out=out_2[0, 4 * q : 4 * q + 4, first:last].bitcast(I32),
+                    in_=out_scale[32 * q : 32 * q + 4, first:last].bitcast(I32),
+                )
+
+        def small_setup():
+            nc.vector.tensor_copy(out=cgain32[:], in_=cgain[:])
+            nc.vector.tensor_tensor(out=cshift32[:], in0=cbias[:], in1=cgain[:], op=ALU.mult)
+            nc.vector.tensor_copy(out=gain_rows32[:], in_=gain_rows[:])
+
+        def turn_src_gain():
+            bank = psum.tile([P, P], F32, name="sbank")
+            nc.tensor.transpose(bank[:], gain_rows32[:], ident[:])
+            nc.scalar.copy(out=sgain_col[:], in_=bank[:, 0:32])
+
+        permute_pool(0)
+        permute_pool(1)
+        turn_banks(0, 4)
+        turned = 4
+        quantize_unit(0)
+        nc.vector.tensor_scalar(out=tgain32[:], in0=tgain[:], scalar1=RS, scalar2=None, op0=ALU.mult)
+        quantize_unit(1, 2)
+        perm_at = PERM
+        scalar_banks = {}
+
+        for k in range(STEPS):
+            n, g = divmod(k, 2)
+            if k < EARLY:
+                correlate(k, scalar_banks.get(k, ()))
+            turn_banks(turned, turned + TURN[k])
+            turned += TURN[k]
+            if k == 2:
+                turn_src_gain()
+            if k >= 4:
+                if k < STEPS - 1:
+                    store_rows(k - 4)
+                round_chunk(k - 4, nc.gpsimd, "rounded", 1, 0, GCOLS)
+            if k >= EARLY:
+                correlate(k, scalar_banks.get(k, ()))
+            if 2 <= k < STEPS - 2:
+                pool_cells(n - 1, 2 * g)
+                pool_cells(n - 1, 2 * g + 1)
+            if k == STEPS - 2:
+                for t in range(PACK):
+                    pool_cells(n - 1, t)
+            if k >= 4 and GCOLS < 2 * P:
+                round_chunk(k - 4, nc.vector, "rounded", 1, GCOLS)
+            if k + 2 < STEPS:
+                quantize_unit(k + 2)
+            for j in perm_at.get(k, ()):
+                permute_pool(j)
+            if k == 0:
+                small_setup()
+            quantize_corr(k)
+            if k >= 4:
+                quantize_chunk(k - 4)
+                if k % 2 == 1 and k < STEPS - 1:
+                    store_words(k - 5, k - 3)
+        store_rows(11)
+        store_rows(12)
+        store_words(10, 12)
+        store_scales(0, 3 * SRC, [nc.sync] * 4)
+        round_chunk(12, nc.vector, "last", 2)
+        round_chunk(13, nc.vector, "last", 2)
+        quantize_chunk(12)
+        for t in range(PACK):
+            pool_cells(HALVES - 1, t)
+        store_rows(13)
+        quantize_chunk(13)
+        store_words(12, 14)
+        round_chunk(14, nc.vector, "last", 2)
+        round_chunk(15, nc.vector, "last", 2)
+        store_rows(14)
+        quantize_chunk(14)
+        store_rows(15, whole=False)
+        quantize_chunk(15)
+        store_words(14, 16)
+        store_scales(3 * SRC, G * SRC, [nc.sync, nc.scalar, nc.sync, nc.scalar])

@@ -20,14 +20,19 @@ ALU = mybir.AluOpType
 P = 128
 PACK = 4
 SPAN = P * PACK
-HALVES = 2 * G
-STEPS = 2 * HALVES
-GROUPED_BUFS = 7
-TURN = (4, 4, 3, 3, 2, 1, 2, 1, 2, 1, 2, 1, 1, 1, 0, 0)
-GCOLS = 192
-EARLY = 3
-PERM = {0: (2, 3, 8), 1: (9, 10, 11), 2: (4, 5), 3: (6, 7)}
+CHUNK = 2 * P
+PERIODS = G * SRC // SPAN
+LAST = PERIODS - 1
+UNITS = 4 * G
+PASSES = G * TGT // SPAN
 RS = 1.0 / math.sqrt(D)
+
+SRC_GAIN, CELL_GAIN, CELL_BIAS, CONSTS = 0, 32, 48, 64
+
+OPENING_TURNS = 21
+TURNS = {2: (2, 3), 3: (1, 2), 4: (1, 2), 5: (0, 0)}
+
+SHARED_SLOT_PERIODS = 5
 
 
 def tile_grouped_correlation_dense_pooling_k7_kernel(
@@ -37,317 +42,433 @@ def tile_grouped_correlation_dense_pooling_k7_kernel(
     with ExitStack() as ctx:
         keep = ctx.enter_context(tc.tile_pool(name="keep", bufs=1))
         work = ctx.enter_context(tc.tile_pool(name="work", bufs=2))
-        psum = ctx.enter_context(tc.psum_pool(name="psum", bufs=4))
+        psum = ctx.enter_context(tc.psum_pool(name="psum", bufs=8))
         ctx.enter_context(tc.manual_schedule())
 
         ident = keep.tile([P, P], F32, name="ident")
         make_identity(nc, ident[:])
-        pool_scale_raw = keep.tile([P, HALVES, CELLS], U8, name="pool_scale_raw", align_bytes=64)
-        nc.gpsimd.memset(pool_scale_raw[:].rearrange("p g n -> p (g n)").bitcast(I32), 0)
-        gain_rows = keep.tile([P, P], BF16, name="gain_rows")
-        nc.gpsimd.memset(gain_rows[:], 0.0)
+        pool_scale = keep.tile([P, PASSES, CELLS], U8, name="pool_scale", align_bytes=64)
+        nc.gpsimd.memset(pool_scale[:].rearrange("p g n -> p (g n)").bitcast(I32), 0)
+        const_rows = keep.tile([P, P], BF16, name="const_rows")
+        nc.gpsimd.memset(const_rows[:], 0.0)
 
         raw = {}
 
         def load_unit(u, parts=1):
             h, kind = divmod(u, 4)
-            rows = slice(SPAN * (kind // 2), SPAN * (kind // 2 + 1))
-            raw[u] = work.tile([P, PACK, D], BF16, name="raw", bufs=12)
+            pixels = slice(SPAN * (kind // 2), SPAN * (kind // 2 + 1))
+            raw[u] = work.tile([P, PACK, D], BF16, name="raw", bufs=10)
             if kind % 2 == 0:
-                view = tgt_feat[h, rows, :].rearrange("(m s) k -> m s k", s=PACK)
+                view = tgt_feat[h, pixels, :].rearrange("(m s) k -> m s k", s=PACK)
             else:
-                view = src_feat[h, rows, :].rearrange("(s m) k -> m s k", s=PACK)
+                view = src_feat[h, pixels, :].rearrange("(s m) k -> m s k", s=PACK)
             step = PACK // parts
             for s in range(0, PACK, step):
                 nc.sync.dma_start(out=raw[u][:, s : s + step, :], in_=view[:, s : s + step, :])
 
-        pool_raw = keep.tile([P, HALVES, 2 * CELLS], U8, name="pool_raw", align_bytes=64)
-        tgain = keep.tile([P, HALVES, PACK], BF16, name="tgain")
-        cbias = keep.tile([P, G, PACK], BF16, name="cbias")
-        cgain = keep.tile([P, G, PACK], BF16, name="cgain")
-        sgain_all = keep.tile([P, G * SRC], BF16, name="sgain_all")
+        pool_codes = keep.tile([P, PASSES, 2 * CELLS], U8, name="pool_codes", align_bytes=64)
+        tgain = keep.tile([P, PASSES, PACK], BF16, name="tgain")
 
-        def load_pool_words(g0, g1):
+        def load_pool_words(first, last):
             nc.sync.dma_start(
-                out=pool_raw[:, g0:g1, :].bitcast(I32),
-                in_=pool_words[g0:g1].rearrange("g p n -> p g n").bitcast(I32),
+                out=pool_codes[:, first:last, :].bitcast(I32),
+                in_=pool_words[first:last].rearrange("g p n -> p g n").bitcast(I32),
             )
 
-        load_unit(0, 2)
-        load_pool_words(0, 2)
-        load_unit(1, 2)
-        nc.sync.dma_start(out=tgain[:], in_=tgt_gain.rearrange("h (g p t) -> p (h g) t", p=P, t=PACK))
+        load_unit(0, parts=2)
+        load_unit(1, parts=2)
         load_unit(2)
-        load_pool_words(2, 4)
-        for q in range(4):
-            nc.sync.dma_start(
-                out=pool_scale_raw[32 * q : 32 * q + 4, :, :].bitcast(I32),
-                in_=pool_scales[:, 4 * q : 4 * q + 4, :].rearrange("g r n -> r g n").bitcast(I32),
-            )
-        nc.sync.dma_start(out=cbias[:], in_=cell_bias.rearrange("h (p t) -> p h t", t=PACK))
-        nc.sync.dma_start(out=cgain[:], in_=cell_gain.rearrange("h (p t) -> p h t", t=PACK))
-        nc.sync.dma_start(out=gain_rows[0:32, :], in_=src_gain.rearrange("h (b m) -> (h b) m", m=P))
+        nc.sync.dma_start(out=tgain[:], in_=tgt_gain.rearrange("h (g p t) -> p (h g) t", p=P, t=PACK))
         load_unit(3)
+        for first, last, vector in (
+            (SRC_GAIN, CELL_GAIN, src_gain),
+            (CELL_GAIN, CELL_BIAS, cell_gain),
+            (CELL_BIAS, CONSTS, cell_bias),
+        ):
+            nc.sync.dma_start(out=const_rows[first:last, :], in_=vector.rearrange("h (b m) -> (h b) m", m=P))
         load_unit(4)
-        load_pool_words(4, 8)
+        for quad in range(4):
+            nc.sync.dma_start(
+                out=pool_scale[32 * quad : 32 * quad + 4, :, :].bitcast(I32),
+                in_=pool_scales[:, 4 * quad : 4 * quad + 4, :].rearrange("g r n -> r g n").bitcast(I32),
+            )
+        load_pool_words(0, 2)
         load_unit(5)
-        for h in range(G):
-            nc.sync.dma_start(out=sgain_all[:, SRC * h : SRC * (h + 1)], in_=src_gain[h].partition_broadcast(P))
-            for u in range(6 + 3 * h, min(9 + 3 * h, 4 * G)):
-                load_unit(u)
+        load_unit(6)
+        load_pool_words(2, PASSES)
+        for u in range(7, UNITS):
+            load_unit(u)
+        last_bias = keep.tile([P, CELLS], BF16, name="last_bias")
+        last_gain = keep.tile([P, CELLS], BF16, name="last_gain")
+        nc.sync.dma_start(out=last_bias[:], in_=cell_bias[G - 1].partition_broadcast(P))
+        nc.sync.dma_start(out=last_gain[:], in_=cell_gain[G - 1].partition_broadcast(P))
 
-        pool_codes = keep.tile([P, HALVES, 2 * CELLS], U8, name="pool_codes", align_bytes=64)
-        pool_scale = keep.tile([P, HALVES, CELLS], U8, name="pool_scale", align_bytes=64)
         out_codes = keep.tile([P, G * SRC], U32, name="out_codes", align_bytes=64)
         out_scale = keep.tile([P, G * SRC], U8, name="out_scale", align_bytes=64)
-        tgain32 = keep.tile([P, HALVES, PACK], F32, name="tgain32")
-        cgain32 = keep.tile([P, G, PACK], F32, name="cgain32")
-        cshift32 = keep.tile([P, G, PACK], F32, name="cshift32")
-        gain_rows32 = keep.tile([P, P], F32, name="gain_rows32")
-        sgain_col = keep.tile([P, 32], F32, name="sgain_col")
+        cell_shift = keep.tile([P, CONSTS - CELL_BIAS], F32, name="cell_shift")
+        const_rows32 = keep.tile([P, P], F32, name="const_rows32")
+        consts = keep.tile([P, CONSTS], F32, name="consts")
 
-        def permute_pool(j):
-            if j < HALVES:
-                g = j
-                nc.vector.tensor_copy(
-                    out=pool_codes[:, g, :].rearrange("p (t m b) -> p t m b", t=PACK, b=2),
-                    in_=pool_raw[:, g, :].rearrange("p (m t b) -> p t m b", t=PACK, b=2),
-                )
-            else:
-                h = j - HALVES
-                nc.vector.tensor_copy(
-                    out=pool_scale[:, 2 * h : 2 * h + 2, :].rearrange("p g (t m) -> p g t m", t=PACK),
-                    in_=pool_scale_raw[:, 2 * h : 2 * h + 2, :].rearrange("p g (m t) -> p g t m", t=PACK),
-                )
+        def widen_consts():
+            nc.vector.tensor_copy(out=const_rows32[:], in_=const_rows[:])
+
+        def turn_consts():
+            bank = psum.tile([P, P], F32, name="bank")
+            nc.tensor.transpose(bank[:], const_rows32[:], ident[:])
+            nc.scalar.copy(out=consts[:], in_=bank[:, 0:CONSTS])
+
+        def make_cell_shift():
+            nc.vector.tensor_tensor(
+                out=cell_shift[:], in0=consts[:, CELL_BIAS:CONSTS], in1=consts[:, CELL_GAIN:CELL_BIAS], op=ALU.mult
+            )
 
         grouped, feat_codes, feat_scale = {}, {}, {}
 
-        def turn_banks(first_bank, last_bank):
-            for j in range(first_bank, last_bank):
-                u, b = divmod(j, 2)
-                words = raw[u][:].rearrange("p s k -> p (s k)").bitcast(F32)
-                if b == 0:
-                    grouped[u] = work.tile([P, SPAN * PACK], BF16, name="grouped", bufs=GROUPED_BUFS, align_bytes=64)
-                pairs = grouped[u][:].bitcast(F32).rearrange("p (c e) -> p c e", e=2)
-                bank = psum.tile([P, 2, 2 * P], F32, name="sbank")
-                for s in range(2):
-                    for e in range(2):
-                        first = (2 * b + s) * (D // 2) + e
-                        nc.tensor.transpose(
-                            bank[:, e, s * P : (s + 1) * P], words[:, first : first + D // 2 - e : 2], ident[:]
-                        )
-                nc.scalar.copy(out=pairs[:, 2 * P * b : 2 * P * (b + 1), :], in_=bank[:].rearrange("p e c -> p c e"))
+        def turn_features(j, on_vector=False):
+            u, b = divmod(j, 2)
+            m, quarter = divmod(j, 4)
+            words = raw[u][:].rearrange("p s k -> p (s k)").bitcast(F32)
+            if quarter == 0:
+                grouped[m] = work.tile([P, 2 * SPAN * PACK], BF16, name="grouped", bufs=4, align_bytes=64)
+            pairs = grouped[m][:].bitcast(F32).rearrange("p (c e) -> p c e", e=2)
+            bank = psum.tile([P, 2, CHUNK], F32, name="bank")
+            for s in range(2):
+                for e in range(2):
+                    word = (2 * b + s) * (D // 2) + e
+                    nc.tensor.transpose(
+                        bank[:, e, s * P : (s + 1) * P], words[:, word : word + D // 2 - e : 2], ident[:]
+                    )
+            copy = nc.vector.tensor_copy if on_vector else nc.scalar.copy
+            copy(out=pairs[:, CHUNK * quarter : CHUNK * (quarter + 1), :], in_=bank[:].rearrange("p e c -> p c e"))
 
-        def quantize_unit(u, parts=1):
-            feat_codes[u] = work.tile([P, SPAN], U32, name="feat_codes", bufs=6, align_bytes=64)
-            feat_scale[u] = work.tile([P, SPAN], U8, name="feat_scale", bufs=6, align_bytes=64)
-            step = SPAN // parts
-            for c in range(0, SPAN, step):
-                nc.vector.quantize_mx(
-                    out=feat_codes[u][:, c : c + step].bitcast(FP8X4),
-                    scales=feat_scale[u][:, c : c + step],
-                    in_=grouped[u][:, PACK * c : PACK * (c + step)],
-                )
+        def quantize_features(m, first=0, last=4):
+            if first == 0:
+                feat_codes[m] = work.tile([P, 2 * SPAN], U32, name="feat_codes", bufs=4, align_bytes=64)
+                feat_scale[m] = work.tile([P, 2 * SPAN], U8, name="feat_scale", bufs=4, align_bytes=64)
+            cols = slice(CHUNK * first, CHUNK * last)
+            nc.vector.quantize_mx(
+                out=feat_codes[m][:, cols].bitcast(FP8X4),
+                scales=feat_scale[m][:, cols],
+                in_=grouped[m][:, PACK * CHUNK * first : PACK * CHUNK * last],
+            )
 
         corr, corr_codes, corr_scale = {}, {}, {}
 
-        def correlate(k, by_scalar):
-            n, g = divmod(k, 2)
+        def correlate(n, b):
             h, half = divmod(n, 2)
-            ut, us = 4 * h + 2 * g, 4 * h + 2 * half + 1
-            corr[k] = work.tile([P, SPAN, PACK], BF16, name="corr", bufs=2, align_bytes=64)
-            for b in range(4):
-                cols = slice(P * b, P * (b + 1))
-                bank = psum.tile([P, PACK, P], F32, name="vbank")
-                for t in range(PACK):
-                    tcols = slice(P * t, P * (t + 1))
-                    nc.tensor.matmul_mx(
-                        out=bank[:, t, :],
-                        lhsT=feat_codes[ut][:, tcols].bitcast(FP8X4),
-                        lhsT_scale=feat_scale[ut][:, tcols],
-                        rhs=feat_codes[us][:, cols].bitcast(FP8X4),
-                        rhs_scale=feat_scale[us][:, cols],
-                        start=True,
-                        stop=True,
-                    )
-                if b in by_scalar:
-                    for t in range(PACK):
-                        nc.scalar.activation(
-                            out=corr[k][:, cols, t],
-                            in_=bank[:, t, :],
-                            func=ACT.Copy,
-                            scale=tgain32[:, 2 * h + g, t : t + 1],
-                        )
-                    continue
-                nc.vector.scalar_tensor_tensor(
-                    out=corr[k][:, cols, :],
-                    in0=bank[:].rearrange("p t i -> p i t"),
-                    scalar=RS,
-                    in1=tgain[:, 2 * h + g, :].unsqueeze(1).to_broadcast([P, P, PACK]),
-                    op0=ALU.mult,
-                    op1=ALU.mult,
+            if b == 0:
+                corr[n] = work.tile([P, 2 * SPAN, PACK], BF16, name="corr", bufs=2, align_bytes=64)
+            g, block = divmod(b, 4) if n < LAST else (b % 2, b // 2)
+            tgt_tile, src_tile = 2 * h + g, 2 * h + half
+            src_cols = slice(SPAN + P * block, SPAN + P * (block + 1))
+            bank = psum.tile([P, PACK, P], F32, name="bank")
+            for t in range(PACK):
+                tgt_cols = slice(P * t, P * (t + 1))
+                nc.tensor.matmul_mx(
+                    out=bank[:, t, :],
+                    lhsT=feat_codes[tgt_tile][:, tgt_cols].bitcast(FP8X4),
+                    lhsT_scale=feat_scale[tgt_tile][:, tgt_cols],
+                    rhs=feat_codes[src_tile][:, src_cols].bitcast(FP8X4),
+                    rhs_scale=feat_scale[src_tile][:, src_cols],
+                    start=True,
+                    stop=True,
                 )
-
-        def quantize_corr(k):
-            corr_codes[k] = work.tile([P, SPAN], U32, name="corr_codes", bufs=4, align_bytes=64)
-            corr_scale[k] = work.tile([P, SPAN], U8, name="corr_scale", bufs=4, align_bytes=64)
-            nc.vector.quantize_mx(
-                out=corr_codes[k][:].bitcast(FP8X4),
-                scales=corr_scale[k][:],
-                in_=corr[k][:].rearrange("p i t -> p (i t)"),
+            nc.vector.scalar_tensor_tensor(
+                out=corr[n][:, P * b : P * (b + 1), :],
+                in0=bank[:].rearrange("p t i -> p i t"),
+                scalar=RS,
+                in1=tgain[:, 2 * h + g, :].unsqueeze(1).to_broadcast([P, P, PACK]),
+                op0=ALU.mult,
+                op1=ALU.mult,
             )
 
-        pooled = {}
+        def quantize_corr(n, first=0, last=8):
+            if first == 0:
+                corr_codes[n] = work.tile([P, 2 * SPAN], U32, name="corr_codes", bufs=2, align_bytes=64)
+                corr_scale[n] = work.tile([P, 2 * SPAN], U8, name="corr_scale", bufs=2, align_bytes=64)
+            cols = slice(P * first, P * last)
+            nc.vector.quantize_mx(
+                out=corr_codes[n][:, cols].bitcast(FP8X4),
+                scales=corr_scale[n][:, cols],
+                in_=corr[n][:, cols, :].rearrange("p i t -> p (i t)"),
+            )
 
-        def pool_cells(n, t):
+        pooled, rows = {}, {}
+
+        def pool_cells(n, j):
             h = n // 2
-            if t == 0:
+            if j == 0:
                 pooled[n] = work.tile([P, PACK, SPAN], F32, name="pooled", bufs=3)
-            bank = psum.tile([P, SPAN], F32, name="sbank")
+            bank = psum.tile([P, SPAN], F32, name="bank")
             for g in range(2):
                 nc.tensor.matmul_mx(
                     out=bank[:],
-                    lhsT=pool_codes[:, 2 * h + g, 2 * P * t : 2 * P * (t + 1)].bitcast(FP4X4),
-                    lhsT_scale=pool_scale[:, 2 * h + g, P * t : P * (t + 1)],
-                    rhs=corr_codes[2 * n + g][:].bitcast(FP8X4),
-                    rhs_scale=corr_scale[2 * n + g][:],
+                    lhsT=pool_codes[:, 2 * h + g, 2 * P * j : 2 * P * (j + 1)].bitcast(FP4X4),
+                    lhsT_scale=pool_scale[:, 2 * h + g, P * j : P * (j + 1)],
+                    rhs=corr_codes[n][:, SPAN * g : SPAN * (g + 1)].bitcast(FP8X4),
+                    rhs_scale=corr_scale[n][:, SPAN * g : SPAN * (g + 1)],
                     start=(g == 0),
                     stop=(g == 1),
                 )
+            col = 4 * h + j
             nc.scalar.activation(
-                out=pooled[n][:, t, :],
+                out=pooled[n][:, j, :],
                 in_=bank[:],
                 func=ACT.Identity,
-                bias=cshift32[:, h, t : t + 1],
-                scale=cgain32[:, h, t : t + 1],
+                bias=cell_shift[:, col : col + 1],
+                scale=consts[:, CELL_GAIN + col : CELL_GAIN + col + 1],
             )
 
-        def store_rows(c, whole=True):
+        def turn_rows(c, s, on_vector=False):
             n, part = divmod(c, 2)
-            y = work.tile([P, 2, CELLS], F32, name="y", bufs=5)
+            if s == 0:
+                rows[c] = work.tile([P, 2, CELLS], F32, name="rows", bufs=5)
+            block = 2 * part + s
+            bank = psum.tile([P, PACK, P], F32, name="bank")
+            for j in range(PACK):
+                nc.tensor.transpose(bank[:, j, :], pooled[n][:, j, P * block : P * (block + 1)], ident[:])
+            gain = consts[:, SRC_GAIN + 2 * c + s : SRC_GAIN + 2 * c + s + 1]
+            flat = bank[:].rearrange("i j p -> i (j p)")
+            if on_vector:
+                nc.vector.tensor_scalar(out=rows[c][:, s, :], in0=flat, scalar1=gain, scalar2=None, op0=ALU.mult)
+            else:
+                nc.scalar.activation(out=rows[c][:, s, :], in_=flat, func=ACT.Copy, scale=gain)
+
+        def store_rows(c, first=0, last=2):
+            h, row = divmod(CHUNK * c, SRC)
+            nc.sync.dma_start(
+                out=out_0[h, row + P * first : row + P * last, :].rearrange("(s m) c -> m s c", m=P),
+                in_=rows[c][:, first:last, :],
+            )
+
+        direct, shifted = {}, {}
+
+        def pool_direct(block):
+            direct[block] = psum.tile([P, CELLS], F32, name="bank")
+            for g in range(2):
+                cols = slice(P * (2 * block + g), P * (2 * block + g + 1))
+                nc.tensor.matmul_mx(
+                    out=direct[block][:],
+                    lhsT=corr_codes[LAST][:, cols].bitcast(FP8X4),
+                    lhsT_scale=corr_scale[LAST][:, cols],
+                    rhs=pool_codes[:, PASSES - 2 + g, :].bitcast(FP4X4),
+                    rhs_scale=pool_scale[:, PASSES - 2 + g, :],
+                    start=(g == 0),
+                    stop=(g == 1),
+                )
+
+        def add_bias(block):
+            shifted[block] = work.tile([P, CELLS], F32, name="shifted", bufs=4)
+            nc.vector.tensor_tensor(out=shifted[block][:], in0=direct[block][:], in1=last_bias[:], op=ALU.add)
+
+        def apply_gains(block):
+            c, s = 2 * LAST + block // 2, block % 2
+            if s == 0:
+                rows[c] = work.tile([P, 2, CELLS], F32, name="rows", bufs=5)
+            nc.vector.scalar_tensor_tensor(
+                out=rows[c][:, s, :],
+                in0=shifted[block][:],
+                scalar=consts[:, SRC_GAIN + 2 * c + s : SRC_GAIN + 2 * c + s + 1],
+                in1=last_gain[:],
+                op0=ALU.mult,
+                op1=ALU.mult,
+            )
+
+        paired, rounded = {}, {}
+
+        def plane_tile(shape, n, name):
+            if n < SHARED_SLOT_PERIODS:
+                return work.tile(shape, BF16, name="shared_slot", bufs=1, align_bytes=64)
+            return work.tile(shape, BF16, name=name, bufs=2, align_bytes=64)
+
+        def round_rows(c, engine):
+            n, part = divmod(c, 2)
+            if n not in paired:
+                paired[n] = plane_tile([P, 2, 2, CHUNK, 2], n, "paired")
+            out = paired[n][:, part]
+            in_ = rows[c][:].rearrange("i s (p u e) -> i u (s p) e", u=2, e=2)
+            if engine == "vector":
+                nc.vector.tensor_copy(out=out, in_=in_)
+            elif engine == "scalar":
+                nc.scalar.copy(out=out, in_=in_)
+            else:
+                nc.gpsimd.tensor_scalar(out=out, in0=in_, scalar1=1.0, scalar2=0.0, op0=ALU.mult, op1=ALU.add)
+
+        def turn_pairs(c):
+            n, part = divmod(c, 2)
+            words = paired[n][:, part].rearrange("i u w e -> i u (w e)").bitcast(F32)
+            if n not in rounded:
+                rounded[n] = plane_tile([P, SPAN * PACK], n, "rounded")
+            bank = psum.tile([P, 2, CHUNK], F32, name="bank")
             for s in range(2):
-                b = 2 * part + s
-                bank = psum.tile([P, PACK, P], F32, name="sbank")
-                for t in range(PACK):
-                    nc.tensor.transpose(bank[:, t, :], pooled[n][:, t, P * b : P * (b + 1)], ident[:])
-                nc.scalar.activation(
-                    out=y[:, s, :].rearrange("i (p t) -> i p t", t=PACK),
-                    in_=bank[:].rearrange("i t p -> i p t"),
-                    func=ACT.Copy,
-                    scale=sgain_col[:, 4 * n + b : 4 * n + b + 1],
-                )
-                h, first = divmod(2 * P * c, SRC)
-                if not whole:
-                    nc.sync.dma_start(out=out_0[h, first + P * s : first + P * (s + 1), :], in_=y[:, s, :])
-            if whole:
-                nc.sync.dma_start(
-                    out=out_0[h, first : first + 2 * P, :].rearrange("(s m) c -> m s c", s=2), in_=y[:]
-                )
+                for u in range(2):
+                    nc.tensor.transpose(bank[:, u, s * P : (s + 1) * P], words[:, u, s * P : (s + 1) * P], ident[:])
+            pairs = rounded[n][:].bitcast(F32).rearrange("p (i u) -> p i u", u=2)
+            nc.scalar.copy(out=pairs[:, CHUNK * part : CHUNK * (part + 1), :], in_=bank[:].rearrange("p u i -> p i u"))
 
-        rounded = {}
-
-        def round_chunk(c, engine, name, bufs, first=0, last=2 * P):
-            n, part = divmod(c, 2)
-            if first == 0:
-                rounded[c] = work.tile([P, 2 * P, PACK], BF16, name=name, bufs=bufs, align_bytes=64)
-            engine.tensor_tensor(
-                out=rounded[c][:, first:last, :],
-                in0=pooled[n][:, :, 2 * P * part + first : 2 * P * part + last].rearrange("p t i -> p i t"),
-                in1=sgain_all[:, 2 * P * c + first : 2 * P * c + last].unsqueeze(2).to_broadcast([P, last - first, PACK]),
-                op=ALU.mult,
+        def quantize_planes(n, first=0, last=2):
+            cols = slice(SPAN * n + CHUNK * first, SPAN * n + CHUNK * last)
+            nc.vector.quantize_mx(
+                out=out_codes[:, cols].bitcast(FP8X4),
+                scales=out_scale[:, cols],
+                in_=rounded[n][:, PACK * CHUNK * first : PACK * CHUNK * last],
             )
 
         words_out = out_1[0].rearrange("p m t -> p (m t)").bitcast(I32)
 
-        def quantize_chunk(c):
-            cols = slice(2 * P * c, 2 * P * (c + 1))
-            nc.vector.quantize_mx(
-                out=out_codes[:, cols].bitcast(FP8X4),
-                scales=out_scale[:, cols],
-                in_=rounded[c][:].rearrange("p i t -> p (i t)"),
-            )
-
         def store_words(first, last):
-            cols = slice(2 * P * first, 2 * P * last)
+            cols = slice(CHUNK * first, CHUNK * last)
             nc.sync.dma_start(out=words_out[:, cols], in_=out_codes[:, cols].bitcast(I32))
 
-        def store_scales(first, last, engines):
-            for q in range(4):
-                engines[q].dma_start(
-                    out=out_2[0, 4 * q : 4 * q + 4, first:last].bitcast(I32),
-                    in_=out_scale[32 * q : 32 * q + 4, first:last].bitcast(I32),
+        def store_scales(first, last, queues):
+            for quad in range(4):
+                queues[quad % len(queues)].dma_start(
+                    out=out_2[0, 4 * quad : 4 * quad + 4, first:last].bitcast(I32),
+                    in_=out_scale[32 * quad : 32 * quad + 4, first:last].bitcast(I32),
                 )
 
-        def small_setup():
-            nc.vector.tensor_copy(out=cgain32[:], in_=cgain[:])
-            nc.vector.tensor_tensor(out=cshift32[:], in0=cbias[:], in1=cgain[:], op=ALU.mult)
-            nc.vector.tensor_copy(out=gain_rows32[:], in_=gain_rows[:])
+        def each(call, first, last, *lead):
+            for index in range(first, last):
+                call(*lead, index)
 
-        def turn_src_gain():
-            bank = psum.tile([P, P], F32, name="sbank")
-            nc.tensor.transpose(bank[:], gain_rows32[:], ident[:])
-            nc.scalar.copy(out=sgain_col[:], in_=bank[:, 0:32])
+        each(turn_features, 0, 3)
+        quantize_features(0, 0, 2)
+        turn_features(3)
+        turn_features(4, on_vector=True)
+        quantize_features(0, 2, 4)
+        each(turn_features, 5, 7)
+        quantize_features(1, 0, 2)
+        turn_features(7)
+        widen_consts()
+        each(correlate, 0, 4, 0)
+        turn_features(8)
+        correlate(0, 4)
+        quantize_features(1, 2, 4)
+        each(correlate, 5, 7, 0)
+        turn_features(9)
+        turn_consts()
+        turn_features(10)
+        correlate(0, 7)
+        correlate(1, 0)
+        each(turn_features, 11, 13)
+        quantize_corr(0)
+        turn_features(13)
+        each(correlate, 1, 3, 1)
+        make_cell_shift()
+        each(correlate, 3, 5, 1)
+        each(pool_cells, 0, 2, 0)
+        each(correlate, 5, 7, 1)
+        turn_features(14)
+        turn_features(15, on_vector=True)
+        turn_features(16)
+        quantize_features(2)
+        turn_features(17)
+        correlate(1, 7)
+        pool_cells(0, 2)
+        quantize_features(3)
+        pool_cells(0, 3)
+        turn_features(18)
+        turn_features(19, on_vector=True)
+        quantize_corr(1)
+        turn_rows(0, 0)
+        turn_features(20)
+        turn_rows(0, 1)
+        store_rows(0)
+        turn_rows(1, 0)
+        turn_rows(1, 1, on_vector=True)
+        store_rows(1)
 
-        permute_pool(0)
-        permute_pool(1)
-        turn_banks(0, 4)
-        turned = 4
-        quantize_unit(0)
-        nc.vector.tensor_scalar(out=tgain32[:], in0=tgain[:], scalar1=RS, scalar2=None, op0=ALU.mult)
-        quantize_unit(1, 2)
-        perm_at = PERM
-        scalar_banks = {}
+        turned = OPENING_TURNS
+        for n in sorted(TURNS):
+            before, after = TURNS[n]
+            rows_first, pairs_first = 2 * (n - 1), 2 * (n - 2)
+            each(correlate, 0, 3, n)
+            round_rows(pairs_first, "gpsimd")
+            each(correlate, 3, 5, n)
+            each(pool_cells, 0, 2, n - 1)
+            each(correlate, 5, 7, n)
+            pool_cells(n - 1, 2)
+            correlate(n, 7)
+            pool_cells(n - 1, 3)
+            each(turn_features, turned, turned + before)
+            round_rows(pairs_first + 1, "gpsimd")
+            turn_pairs(pairs_first)
+            quantize_corr(n)
+            turn_pairs(pairs_first + 1)
+            quantize_features(n + 2)
+            turn_rows(rows_first, 0)
+            turn_rows(rows_first, 1, on_vector=True)
+            quantize_planes(n - 2)
+            store_rows(rows_first)
+            each(turn_rows, 0, 2, rows_first + 1)
+            store_words(pairs_first, pairs_first + 2)
+            each(turn_features, turned + before, turned + before + after)
+            store_rows(rows_first + 1)
+            turned += before + after
 
-        for k in range(STEPS):
-            n, g = divmod(k, 2)
-            if k < EARLY:
-                correlate(k, scalar_banks.get(k, ()))
-            turn_banks(turned, turned + TURN[k])
-            turned += TURN[k]
-            if k == 2:
-                turn_src_gain()
-            if k >= 4:
-                if k < STEPS - 1:
-                    store_rows(k - 4)
-                round_chunk(k - 4, nc.gpsimd, "rounded", 1, 0, GCOLS)
-            if k >= EARLY:
-                correlate(k, scalar_banks.get(k, ()))
-            if 2 <= k < STEPS - 2:
-                pool_cells(n - 1, 2 * g)
-                pool_cells(n - 1, 2 * g + 1)
-            if k == STEPS - 2:
-                for t in range(PACK):
-                    pool_cells(n - 1, t)
-            if k >= 4 and GCOLS < 2 * P:
-                round_chunk(k - 4, nc.vector, "rounded", 1, GCOLS)
-            if k + 2 < STEPS:
-                quantize_unit(k + 2)
-            for j in perm_at.get(k, ()):
-                permute_pool(j)
-            if k == 0:
-                small_setup()
-            quantize_corr(k)
-            if k >= 4:
-                quantize_chunk(k - 4)
-                if k % 2 == 1 and k < STEPS - 1:
-                    store_words(k - 5, k - 3)
+        each(correlate, 0, 3, 6)
+        round_rows(8, "gpsimd")
+        each(correlate, 3, 5, 6)
+        pool_cells(5, 0)
+        correlate(6, 5)
+        round_rows(9, "scalar")
+        pool_cells(5, 1)
+        correlate(6, 6)
+        pool_cells(5, 2)
+        correlate(6, 7)
+        pool_cells(5, 3)
+        each(turn_pairs, 8, 10)
+        correlate(7, 0)
+        each(turn_rows, 0, 2, 10)
+        store_rows(10)
+        turn_rows(11, 0)
+        quantize_corr(6)
+        quantize_planes(4)
+        round_rows(10, "gpsimd")
+        turn_rows(11, 1)
         store_rows(11)
+        store_words(8, 10)
+        each(correlate, 1, 5, 7)
+        pool_cells(6, 0)
+        round_rows(11, "gpsimd")
+        each(pool_cells, 1, 3, 6)
+        each(correlate, 5, 7, 7)
+        pool_cells(6, 3)
+        correlate(7, 7)
+        quantize_corr(7, 0, 4)
+        quantize_corr(7, 4, 8)
+        turn_pairs(10)
+        turn_rows(12, 0)
+        turn_rows(13, 0, on_vector=True)
+        turn_rows(12, 1)
         store_rows(12)
-        store_words(10, 12)
-        store_scales(0, 3 * SRC, [nc.sync] * 4)
-        round_chunk(12, nc.vector, "last", 2)
-        round_chunk(13, nc.vector, "last", 2)
-        quantize_chunk(12)
-        for t in range(PACK):
-            pool_cells(HALVES - 1, t)
+        turn_rows(13, 1)
         store_rows(13)
-        quantize_chunk(13)
-        store_words(12, 14)
-        round_chunk(14, nc.vector, "last", 2)
-        round_chunk(15, nc.vector, "last", 2)
+        pool_direct(0)
+        round_rows(13, "scalar")
+        add_bias(0)
+        each(pool_direct, 1, 4)
+        each(add_bias, 1, 4)
+        round_rows(12, "gpsimd")
+        apply_gains(0)
+        each(turn_pairs, 11, 13)
+        apply_gains(1)
         store_rows(14)
-        quantize_chunk(14)
-        store_rows(15, whole=False)
-        quantize_chunk(15)
-        store_words(14, 16)
-        store_scales(3 * SRC, G * SRC, [nc.sync, nc.scalar, nc.sync, nc.scalar])
+        round_rows(14, "scalar")
+        apply_gains(2)
+        store_rows(15, 0, 1)
+        turn_pairs(13)
+        apply_gains(3)
+        store_rows(15, 1, 2)
+        quantize_planes(5)
+        round_rows(15, "vector")
+        store_words(10, 12)
+        store_scales(0, (G - 1) * SRC, [nc.sync])
+        each(turn_pairs, 14, 16)
+        quantize_planes(6)
+        store_words(12, 14)
+        quantize_planes(7, 0, 1)
+        store_words(14, 15)
+        quantize_planes(7, 1, 2)
+        store_words(15, 16)
+        store_scales((G - 1) * SRC, G * SRC, [nc.sync, nc.scalar])

import math
from contextlib import ExitStack

import concourse.mybir as mybir
from concourse.masks import make_identity

G, SRC, TGT, D, CELLS = 4, 1024, 1024, 512, 512
FLOPS = 2 * G * SRC * TGT * D + 2 * G * SRC * TGT * CELLS

F32 = mybir.dt.float32
BF16 = mybir.dt.bfloat16
I32 = mybir.dt.int32
U32 = mybir.dt.uint32
U8 = mybir.dt.uint8
FP8X4 = mybir.dt.float8_e4m3fn_x4
FP4X4 = mybir.dt.float4_e2m1fn_x4
ACT = mybir.ActivationFunctionType
ALU = mybir.AluOpType

P = 128
PACK = 4
SPAN = P * PACK
CHUNK = 2 * P
PERIODS = G * SRC // SPAN
LAST = PERIODS - 1
UNITS = 4 * G
PASSES = G * TGT // SPAN
RS = 1.0 / math.sqrt(D)

SRC_GAIN, CELL_GAIN, CELL_BIAS, CONSTS = 0, 32, 48, 64

OPENING_TURNS = 21
TURNS = {2: (2, 3), 3: (1, 2), 4: (1, 2), 5: (0, 0)}

SHARED_SLOT_PERIODS = 5


def tile_grouped_correlation_dense_pooling_k7_kernel(
    tc, src_feat, tgt_feat, tgt_gain, pool_words, pool_scales, cell_bias, cell_gain, src_gain, out_0, out_1, out_2
):
    nc = tc.nc
    with ExitStack() as ctx:
        keep = ctx.enter_context(tc.tile_pool(name="keep", bufs=1))
        work = ctx.enter_context(tc.tile_pool(name="work", bufs=2))
        psum = ctx.enter_context(tc.psum_pool(name="psum", bufs=8))
        ctx.enter_context(tc.manual_schedule())

        ident = keep.tile([P, P], F32, name="ident")
        make_identity(nc, ident[:])
        pool_scale = keep.tile([P, PASSES, CELLS], U8, name="pool_scale", align_bytes=64)
        nc.gpsimd.memset(pool_scale[:].rearrange("p g n -> p (g n)").bitcast(I32), 0)
        const_rows = keep.tile([P, P], BF16, name="const_rows")
        nc.gpsimd.memset(const_rows[:], 0.0)

        raw = {}

        def load_unit(u, parts=1):
            h, kind = divmod(u, 4)
            pixels = slice(SPAN * (kind // 2), SPAN * (kind // 2 + 1))
            raw[u] = work.tile([P, PACK, D], BF16, name="raw", bufs=10)
            if kind % 2 == 0:
                view = tgt_feat[h, pixels, :].rearrange("(m s) k -> m s k", s=PACK)
            else:
                view = src_feat[h, pixels, :].rearrange("(s m) k -> m s k", s=PACK)
            step = PACK // parts
            for s in range(0, PACK, step):
                nc.sync.dma_start(out=raw[u][:, s : s + step, :], in_=view[:, s : s + step, :])

        pool_codes = keep.tile([P, PASSES, 2 * CELLS], U8, name="pool_codes", align_bytes=64)
        tgain = keep.tile([P, PASSES, PACK], BF16, name="tgain")

        def load_pool_words(first, last):
            nc.sync.dma_start(
                out=pool_codes[:, first:last, :].bitcast(I32),
                in_=pool_words[first:last].rearrange("g p n -> p g n").bitcast(I32),
            )

        load_unit(0, parts=2)
        load_unit(1, parts=2)
        load_unit(2)
        nc.sync.dma_start(out=tgain[:], in_=tgt_gain.rearrange("h (g p t) -> p (h g) t", p=P, t=PACK))
        load_unit(3)
        for first, last, vector in (
            (SRC_GAIN, CELL_GAIN, src_gain),
            (CELL_GAIN, CELL_BIAS, cell_gain),
            (CELL_BIAS, CONSTS, cell_bias),
        ):
            nc.sync.dma_start(out=const_rows[first:last, :], in_=vector.rearrange("h (b m) -> (h b) m", m=P))
        load_unit(4)
        for quad in range(4):
            nc.sync.dma_start(
                out=pool_scale[32 * quad : 32 * quad + 4, :, :].bitcast(I32),
                in_=pool_scales[:, 4 * quad : 4 * quad + 4, :].rearrange("g r n -> r g n").bitcast(I32),
            )
        load_pool_words(0, 2)
        load_unit(5)
        load_unit(6)
        load_pool_words(2, PASSES)
        for u in range(7, UNITS):
            load_unit(u)
        last_bias = keep.tile([P, CELLS], BF16, name="last_bias")
        last_gain = keep.tile([P, CELLS], BF16, name="last_gain")
        nc.sync.dma_start(out=last_bias[:], in_=cell_bias[G - 1].partition_broadcast(P))
        nc.sync.dma_start(out=last_gain[:], in_=cell_gain[G - 1].partition_broadcast(P))

        out_codes = keep.tile([P, G * SRC], U32, name="out_codes", align_bytes=64)
        out_scale = keep.tile([P, G * SRC], U8, name="out_scale", align_bytes=64)
        cell_shift = keep.tile([P, CONSTS - CELL_BIAS], F32, name="cell_shift")
        const_rows32 = keep.tile([P, P], F32, name="const_rows32")
        consts = keep.tile([P, CONSTS], F32, name="consts")

        def widen_consts():
            nc.vector.tensor_copy(out=const_rows32[:], in_=const_rows[:])

        def turn_consts():
            bank = psum.tile([P, P], F32, name="bank")
            nc.tensor.transpose(bank[:], const_rows32[:], ident[:])
            nc.scalar.copy(out=consts[:], in_=bank[:, 0:CONSTS])

        def make_cell_shift():
            nc.vector.tensor_tensor(
                out=cell_shift[:], in0=consts[:, CELL_BIAS:CONSTS], in1=consts[:, CELL_GAIN:CELL_BIAS], op=ALU.mult
            )

        grouped, feat_codes, feat_scale = {}, {}, {}

        def turn_features(j, on_vector=False):
            u, b = divmod(j, 2)
            m, quarter = divmod(j, 4)
            words = raw[u][:].rearrange("p s k -> p (s k)").bitcast(F32)
            if quarter == 0:
                grouped[m] = work.tile([P, 2 * SPAN * PACK], BF16, name="grouped", bufs=4, align_bytes=64)
            pairs = grouped[m][:].bitcast(F32).rearrange("p (c e) -> p c e", e=2)
            bank = psum.tile([P, 2, CHUNK], F32, name="bank")
            for s in range(2):
                for e in range(2):
                    word = (2 * b + s) * (D // 2) + e
                    nc.tensor.transpose(
                        bank[:, e, s * P : (s + 1) * P], words[:, word : word + D // 2 - e : 2], ident[:]
                    )
            copy = nc.vector.tensor_copy if on_vector else nc.scalar.copy
            copy(out=pairs[:, CHUNK * quarter : CHUNK * (quarter + 1), :], in_=bank[:].rearrange("p e c -> p c e"))

        def quantize_features(m, first=0, last=4):
            if first == 0:
                feat_codes[m] = work.tile([P, 2 * SPAN], U32, name="feat_codes", bufs=4, align_bytes=64)
                feat_scale[m] = work.tile([P, 2 * SPAN], U8, name="feat_scale", bufs=4, align_bytes=64)
            cols = slice(CHUNK * first, CHUNK * last)
            nc.vector.quantize_mx(
                out=feat_codes[m][:, cols].bitcast(FP8X4),
                scales=feat_scale[m][:, cols],
                in_=grouped[m][:, PACK * CHUNK * first : PACK * CHUNK * last],
            )

        corr, corr_codes, corr_scale = {}, {}, {}

        def correlate(n, b):
            h, half = divmod(n, 2)
            if b == 0:
                corr[n] = work.tile([P, 2 * SPAN, PACK], BF16, name="corr", bufs=2, align_bytes=64)
            g, block = divmod(b, 4) if n < LAST else (b % 2, b // 2)
            tgt_tile, src_tile = 2 * h + g, 2 * h + half
            src_cols = slice(SPAN + P * block, SPAN + P * (block + 1))
            bank = psum.tile([P, PACK, P], F32, name="bank")
            for t in range(PACK):
                tgt_cols = slice(P * t, P * (t + 1))
                nc.tensor.matmul_mx(
                    out=bank[:, t, :],
                    lhsT=feat_codes[tgt_tile][:, tgt_cols].bitcast(FP8X4),
                    lhsT_scale=feat_scale[tgt_tile][:, tgt_cols],
                    rhs=feat_codes[src_tile][:, src_cols].bitcast(FP8X4),
                    rhs_scale=feat_scale[src_tile][:, src_cols],
                    start=True,
                    stop=True,
                )
            nc.vector.scalar_tensor_tensor(
                out=corr[n][:, P * b : P * (b + 1), :],
                in0=bank[:].rearrange("p t i -> p i t"),
                scalar=RS,
                in1=tgain[:, 2 * h + g, :].unsqueeze(1).to_broadcast([P, P, PACK]),
                op0=ALU.mult,
                op1=ALU.mult,
            )

        def quantize_corr(n, first=0, last=8):
            if first == 0:
                corr_codes[n] = work.tile([P, 2 * SPAN], U32, name="corr_codes", bufs=2, align_bytes=64)
                corr_scale[n] = work.tile([P, 2 * SPAN], U8, name="corr_scale", bufs=2, align_bytes=64)
            cols = slice(P * first, P * last)
            nc.vector.quantize_mx(
                out=corr_codes[n][:, cols].bitcast(FP8X4),
                scales=corr_scale[n][:, cols],
                in_=corr[n][:, cols, :].rearrange("p i t -> p (i t)"),
            )

        pooled, rows = {}, {}

        def pool_cells(n, j):
            h = n // 2
            if j == 0:
                pooled[n] = work.tile([P, PACK, SPAN], F32, name="pooled", bufs=3)
            bank = psum.tile([P, SPAN], F32, name="bank")
            for g in range(2):
                nc.tensor.matmul_mx(
                    out=bank[:],
                    lhsT=pool_codes[:, 2 * h + g, 2 * P * j : 2 * P * (j + 1)].bitcast(FP4X4),
                    lhsT_scale=pool_scale[:, 2 * h + g, P * j : P * (j + 1)],
                    rhs=corr_codes[n][:, SPAN * g : SPAN * (g + 1)].bitcast(FP8X4),
                    rhs_scale=corr_scale[n][:, SPAN * g : SPAN * (g + 1)],
                    start=(g == 0),
                    stop=(g == 1),
                )
            col = 4 * h + j
            nc.scalar.activation(
                out=pooled[n][:, j, :],
                in_=bank[:],
                func=ACT.Identity,
                bias=cell_shift[:, col : col + 1],
                scale=consts[:, CELL_GAIN + col : CELL_GAIN + col + 1],
            )

        def turn_rows(c, s, on_vector=False):
            n, part = divmod(c, 2)
            if s == 0:
                rows[c] = work.tile([P, 2, CELLS], F32, name="rows", bufs=5)
            block = 2 * part + s
            bank = psum.tile([P, PACK, P], F32, name="bank")
            for j in range(PACK):
                nc.tensor.transpose(bank[:, j, :], pooled[n][:, j, P * block : P * (block + 1)], ident[:])
            gain = consts[:, SRC_GAIN + 2 * c + s : SRC_GAIN + 2 * c + s + 1]
            flat = bank[:].rearrange("i j p -> i (j p)")
            if on_vector:
                nc.vector.tensor_scalar(out=rows[c][:, s, :], in0=flat, scalar1=gain, scalar2=None, op0=ALU.mult)
            else:
                nc.scalar.activation(out=rows[c][:, s, :], in_=flat, func=ACT.Copy, scale=gain)

        def store_rows(c, first=0, last=2):
            h, row = divmod(CHUNK * c, SRC)
            nc.sync.dma_start(
                out=out_0[h, row + P * first : row + P * last, :].rearrange("(s m) c -> m s c", m=P),
                in_=rows[c][:, first:last, :],
            )

        direct, shifted = {}, {}

        def pool_direct(block):
            direct[block] = psum.tile([P, CELLS], F32, name="bank")
            for g in range(2):
                cols = slice(P * (2 * block + g), P * (2 * block + g + 1))
                nc.tensor.matmul_mx(
                    out=direct[block][:],
                    lhsT=corr_codes[LAST][:, cols].bitcast(FP8X4),
                    lhsT_scale=corr_scale[LAST][:, cols],
                    rhs=pool_codes[:, PASSES - 2 + g, :].bitcast(FP4X4),
                    rhs_scale=pool_scale[:, PASSES - 2 + g, :],
                    start=(g == 0),
                    stop=(g == 1),
                )

        def add_bias(block):
            shifted[block] = work.tile([P, CELLS], F32, name="shifted", bufs=4)
            nc.vector.tensor_tensor(out=shifted[block][:], in0=direct[block][:], in1=last_bias[:], op=ALU.add)

        def apply_gains(block):
            c, s = 2 * LAST + block // 2, block % 2
            if s == 0:
                rows[c] = work.tile([P, 2, CELLS], F32, name="rows", bufs=5)
            nc.vector.scalar_tensor_tensor(
                out=rows[c][:, s, :],
                in0=shifted[block][:],
                scalar=consts[:, SRC_GAIN + 2 * c + s : SRC_GAIN + 2 * c + s + 1],
                in1=last_gain[:],
                op0=ALU.mult,
                op1=ALU.mult,
            )

        paired, rounded = {}, {}

        def plane_tile(shape, n, name):
            if n < SHARED_SLOT_PERIODS:
                return work.tile(shape, BF16, name="shared_slot", bufs=1, align_bytes=64)
            return work.tile(shape, BF16, name=name, bufs=2, align_bytes=64)

        def round_rows(c, engine):
            n, part = divmod(c, 2)
            if n not in paired:
                paired[n] = plane_tile([P, 2, 2, CHUNK, 2], n, "paired")
            out = paired[n][:, part]
            in_ = rows[c][:].rearrange("i s (p u e) -> i u (s p) e", u=2, e=2)
            if engine == "vector":
                nc.vector.tensor_copy(out=out, in_=in_)
            elif engine == "scalar":
                nc.scalar.copy(out=out, in_=in_)
            else:
                nc.gpsimd.tensor_scalar(out=out, in0=in_, scalar1=1.0, scalar2=0.0, op0=ALU.mult, op1=ALU.add)

        def turn_pairs(c):
            n, part = divmod(c, 2)
            words = paired[n][:, part].rearrange("i u w e -> i u (w e)").bitcast(F32)
            if n not in rounded:
                rounded[n] = plane_tile([P, SPAN * PACK], n, "rounded")
            bank = psum.tile([P, 2, CHUNK], F32, name="bank")
            for s in range(2):
                for u in range(2):
                    nc.tensor.transpose(bank[:, u, s * P : (s + 1) * P], words[:, u, s * P : (s + 1) * P], ident[:])
            pairs = rounded[n][:].bitcast(F32).rearrange("p (i u) -> p i u", u=2)
            nc.scalar.copy(out=pairs[:, CHUNK * part : CHUNK * (part + 1), :], in_=bank[:].rearrange("p u i -> p i u"))

        def quantize_planes(n, first=0, last=2):
            cols = slice(SPAN * n + CHUNK * first, SPAN * n + CHUNK * last)
            nc.vector.quantize_mx(
                out=out_codes[:, cols].bitcast(FP8X4),
                scales=out_scale[:, cols],
                in_=rounded[n][:, PACK * CHUNK * first : PACK * CHUNK * last],
            )

        words_out = out_1[0].rearrange("p m t -> p (m t)").bitcast(I32)

        def store_words(first, last):
            cols = slice(CHUNK * first, CHUNK * last)
            nc.sync.dma_start(out=words_out[:, cols], in_=out_codes[:, cols].bitcast(I32))

        def store_scales(first, last, queues):
            for quad in range(4):
                queues[quad % len(queues)].dma_start(
                    out=out_2[0, 4 * quad : 4 * quad + 4, first:last].bitcast(I32),
                    in_=out_scale[32 * quad : 32 * quad + 4, first:last].bitcast(I32),
                )

        def each(call, first, last, *lead):
            for index in range(first, last):
                call(*lead, index)

        each(turn_features, 0, 3)
        quantize_features(0, 0, 2)
        turn_features(3)
        turn_features(4, on_vector=True)
        quantize_features(0, 2, 4)
        each(turn_features, 5, 7)
        quantize_features(1, 0, 2)
        turn_features(7)
        widen_consts()
        each(correlate, 0, 4, 0)
        turn_features(8)
        correlate(0, 4)
        quantize_features(1, 2, 4)
        each(correlate, 5, 7, 0)
        turn_features(9)
        turn_consts()
        turn_features(10)
        correlate(0, 7)
        correlate(1, 0)
        each(turn_features, 11, 13)
        quantize_corr(0)
        turn_features(13)
        each(correlate, 1, 3, 1)
        make_cell_shift()
        each(correlate, 3, 5, 1)
        each(pool_cells, 0, 2, 0)
        each(correlate, 5, 7, 1)
        turn_features(14)
        turn_features(15, on_vector=True)
        turn_features(16)
        quantize_features(2)
        turn_features(17)
        correlate(1, 7)
        pool_cells(0, 2)
        quantize_features(3)
        pool_cells(0, 3)
        turn_features(18)
        turn_features(19, on_vector=True)
        quantize_corr(1)
        turn_rows(0, 0)
        turn_features(20)
        turn_rows(0, 1)
        store_rows(0)
        turn_rows(1, 0)
        turn_rows(1, 1, on_vector=True)
        store_rows(1)

        turned = OPENING_TURNS
        for n in sorted(TURNS):
            before, after = TURNS[n]
            rows_first, pairs_first = 2 * (n - 1), 2 * (n - 2)
            each(correlate, 0, 3, n)
            round_rows(pairs_first, "gpsimd")
            each(correlate, 3, 5, n)
            each(pool_cells, 0, 2, n - 1)
            each(correlate, 5, 7, n)
            pool_cells(n - 1, 2)
            correlate(n, 7)
            pool_cells(n - 1, 3)
            each(turn_features, turned, turned + before)
            round_rows(pairs_first + 1, "gpsimd")
            turn_pairs(pairs_first)
            quantize_corr(n)
            turn_pairs(pairs_first + 1)
            quantize_features(n + 2)
            turn_rows(rows_first, 0)
            turn_rows(rows_first, 1, on_vector=True)
            quantize_planes(n - 2)
            store_rows(rows_first)
            each(turn_rows, 0, 2, rows_first + 1)
            store_words(pairs_first, pairs_first + 2)
            each(turn_features, turned + before, turned + before + after)
            store_rows(rows_first + 1)
            turned += before + after

        each(correlate, 0, 3, 6)
        round_rows(8, "gpsimd")
        each(correlate, 3, 5, 6)
        pool_cells(5, 0)
        correlate(6, 5)
        round_rows(9, "scalar")
        pool_cells(5, 1)
        correlate(6, 6)
        pool_cells(5, 2)
        correlate(6, 7)
        pool_cells(5, 3)
        each(turn_pairs, 8, 10)
        correlate(7, 0)
        each(turn_rows, 0, 2, 10)
        store_rows(10)
        turn_rows(11, 0)
        quantize_corr(6)
        quantize_planes(4)
        round_rows(10, "gpsimd")
        turn_rows(11, 1)
        store_rows(11)
        store_words(8, 10)
        each(correlate, 1, 5, 7)
        pool_cells(6, 0)
        round_rows(11, "gpsimd")
        each(pool_cells, 1, 3, 6)
        each(correlate, 5, 7, 7)
        pool_cells(6, 3)
        correlate(7, 7)
        quantize_corr(7, 0, 4)
        quantize_corr(7, 4, 8)
        turn_pairs(10)
        turn_rows(12, 0)
        turn_rows(13, 0, on_vector=True)
        turn_rows(12, 1)
        store_rows(12)
        turn_rows(13, 1)
        store_rows(13)
        pool_direct(0)
        round_rows(13, "scalar")
        add_bias(0)
        each(pool_direct, 1, 4)
        each(add_bias, 1, 4)
        round_rows(12, "gpsimd")
        apply_gains(0)
        each(turn_pairs, 11, 13)
        apply_gains(1)
        store_rows(14)
        round_rows(14, "scalar")
        apply_gains(2)
        store_rows(15, 0, 1)
        turn_pairs(13)
        apply_gains(3)
        store_rows(15, 1, 2)
        quantize_planes(5)
        round_rows(15, "vector")
        store_words(10, 12)
        store_scales(0, (G - 1) * SRC, [nc.sync])
        each(turn_pairs, 14, 16)
        quantize_planes(6)
        store_words(12, 14)
        quantize_planes(7, 0, 1)
        store_words(14, 15)
        quantize_planes(7, 1, 2)
        store_words(15, 16)
        store_scales((G - 1) * SRC, G * SRC, [nc.sync, nc.scalar])
